import numpy as np
import ml_dtypes


def mxq(x, axis, fmt="e4m3"):
    dtype, down = {"e4m3": (ml_dtypes.float8_e4m3fn, 7), "e5m2": (ml_dtypes.float8_e5m2, 14)}[fmt]
    v = np.moveaxis(np.asarray(x, np.float32).astype(ml_dtypes.bfloat16).astype(np.float64), axis, -1)
    blocks = v.reshape(v.shape[:-1] + (-1, 32))
    amax = np.abs(blocks).max(-1, keepdims=True)
    byte = np.maximum(np.where(amax > 0, np.frexp(amax)[1] - 1 + 127, 0) - down, 1)
    scale = np.exp2(byte - 127.0)
    codes = (blocks / scale).astype(np.float32).astype(dtype).astype(np.float64)
    return np.moveaxis((codes * scale).reshape(v.shape), -1, axis)


WIDE = False


def mx_kscale(k):
    if not WIDE:
        return np.ones(k)
    levels = np.array([10, -10, 5, -5, 0])
    if k % 512:
        return np.exp2(np.random.permutation(np.resize(levels, k // 32))).repeat(32)
    a = np.empty((k // 512, 16))
    for p in range(k // 512):
        a[p, :8] = np.random.permutation(np.resize(levels, 8))
        for g in range(8):
            far = levels[np.abs(levels - a[p, g]) >= 10]
            a[p, g + 8] = far[np.random.randint(len(far))]
    return np.exp2(a.ravel()).repeat(32)


def f64(x):
    return np.asarray(x).astype(np.float64)


def striped(idx):
    return np.tile(idx.reshape(-1, 16).T, (8, 1)).astype(np.uint16)


def unstriped(offs):
    return offs[:16].T.reshape(-1).astype(np.int64)


E2M1 = np.array([0.0, 0.5, 1.0, 1.5, 2.0, 3.0, 4.0, 6.0, -0.0, -0.5, -1.0, -1.5, -2.0, -3.0, -4.0, -6.0])


def pack_weight(w, fmt):
    k, n = w.shape
    w = f64(np.asarray(w, np.float32).astype(ml_dtypes.bfloat16)).reshape(k // 32, 32, n)
    amax = np.abs(w).max(1)
    if fmt == "e4m3":
        byte = np.frexp(amax)[1] - 1 + 127 - 7
    else:
        mant, ex = np.frexp(amax / 6.0)
        byte = np.where(mant > 0.5, ex, ex - 1) + 127
    byte = np.clip(np.where(amax > 0, byte, 1), 1, 254)
    scaled = (w * np.exp2(127.0 - byte)[:, None, :]).reshape(k, n).astype(np.float32)
    by_word = np.ascontiguousarray(scaled.reshape(k // 512, 128, 4, n).transpose(0, 1, 3, 2))
    if fmt == "e4m3":
        words = by_word.astype(ml_dtypes.float8_e4m3fn).view(np.uint8)
    else:
        c = by_word.astype(ml_dtypes.float4_e2m1fn).view(np.uint8) & 0xF
        words = (c[..., 0::2] | (c[..., 1::2] << 4)).reshape(k // 512, 128, 2 * n)
    return np.ascontiguousarray(words), np.ascontiguousarray(byte.astype(np.uint8).reshape(k // 512, 16, n))


def unpack_weight(words, scales, fmt):
    g, _, n = scales.shape
    words = np.ascontiguousarray(words).reshape(g, 128, n, -1)
    if fmt == "e4m3":
        vals = words.view(ml_dtypes.float8_e4m3fn).astype(np.float64)
    else:
        nib = np.empty((g, 128, n, 4), np.uint8)
        nib[..., 0::2] = words & 0xF
        nib[..., 1::2] = words >> 4
        vals = E2M1[nib]
    vals = vals * np.repeat(np.exp2(scales.astype(np.float64) - 127.0), 8, axis=1)[..., None]
    return vals.transpose(0, 1, 3, 2).reshape(g * 512, n)


def gelu(v):
    return 0.5 * v * (1.0 + np.tanh(np.sqrt(2.0 / np.pi) * (v + 0.044715 * v**3)))


K, T, S, H, T3, S2, T2 = 1024, 2048, 512, 1024, 1024, 512, 1024


def setup_inputs():
    n = np.random.standard_normal
    s = mx_kscale(K)[:, None]
    u = s
    tab_words, tab_scales = pack_weight(n((K, T)) * s, "e4m3")
    tab2_words, tab2_scales = pack_weight(n((H, T3)) / u / np.sqrt(H), "e4m3")
    w4_words, w4_scales = pack_weight(n((K, H)) / s * u.T / np.sqrt(K), "e2m1")
    return {
        "tab_words": tab_words, "tab_scales": tab_scales,
        "offs": striped(np.random.permutation(T)[:S]),
        "tab2_words": tab2_words, "tab2_scales": tab2_scales,
        "offs2": striped(np.random.permutation(T3)[:S2]),
        "offs3": striped(np.random.permutation(T2)[:S]),
        "w1": (n((K, H)) / s * u.T / np.sqrt(K)).astype(np.float32),
        "w4_words": w4_words, "w4_scales": w4_scales,
        "cap": (0.5 * n(H) * u[:, 0]).astype(np.float32),
        "base": (0.5 * n(H) * u[:, 0]).astype(np.float32),
        "arena": (1.2 * n((S2, S))).astype(np.float32),
        "page1": (0.7 * n((S2, T2))).astype(np.float32),
        "wgo": np.exp(0.3 * n((128, S))).astype(np.float32),
    }


def reference(tab_words, tab_scales, offs, tab2_words, tab2_scales, offs2, offs3,
              w1, w4_words, w4_scales, cap, base, arena, page1, wgo):
    v = unpack_weight(tab_words, tab_scales, "e4m3")[:, unstriped(offs)]
    v2 = unpack_weight(tab2_words, tab2_scales, "e4m3")[:, unstriped(offs2)]
    w4 = unpack_weight(w4_words, w4_scales, "e2m1")
    f1 = mxq(f64(w1), 0, "e4m3").T @ v
    f2 = w4.T @ v
    h = np.minimum(f1, f64(cap)[:, None]) + np.maximum(f2, f64(base)[:, None])
    e = v2.T @ mxq(h, 0, "e4m3")
    d = v2.T @ v
    score = np.tanh(e * f64(arena) + d)
    out = f64(page1).copy()
    out[:, unstriped(offs3)] = np.tile(f64(wgo), (S2 // 128, 1)) * score
    return out

@@ -1,0 +1,230 @@
+from contextlib import ExitStack
+
+import concourse.mybir as mybir
+
+F32 = mybir.dt.float32
+BF16 = mybir.dt.bfloat16
+I32 = mybir.dt.int32
+U32 = mybir.dt.uint32
+U16 = mybir.dt.uint16
+U8 = mybir.dt.uint8
+FP8X4 = mybir.dt.float8_e4m3fn_x4
+FP4X4 = mybir.dt.float4_e2m1fn_x4
+ALU = mybir.AluOpType
+ACT = mybir.ActivationFunctionType
+
+P = 128
+PACK = 4
+K_PASS = P * PACK
+PASSES = 2
+T, T3, S, S2, T2 = 2048, 1024, 512, 512, 1024
+M_TILES = S2 // P
+FLOPS = 3221225472
+
+
+def tile_list_bull_ride_scores_kernel(
+    tc, tab_words, tab_scales, offs, tab2_words, tab2_scales, offs2, offs3,
+    w1, w4_words, w4_scales, cap, base, arena, page1, wgo, out,
+):
+    nc = tc.nc
+    with ExitStack() as ctx:
+        keep = ctx.enter_context(tc.tile_pool(name="keep", bufs=1))
+        ring = ctx.enter_context(tc.tile_pool(name="ring", bufs=2))
+        psum = ctx.enter_context(tc.psum_pool(name="psum", bufs=1))
+
+        def held(shape, dtype, name):
+            return keep.tile(shape, dtype, name=name, align_bytes=64)
+
+        ride_list = held([P, S // 16], U16, "ride_list")
+        bull_list = held([P, S2 // 16], U16, "bull_list")
+        page_list = held([P, S // 16], U16, "page_list")
+        tab_sb = [held([P, T], I32, "tab_sb%d" % a) for a in range(PASSES)]
+        tab2_sb = [held([P, T3], I32, "tab2_sb%d" % a) for a in range(PASSES)]
+        tab_sc = held([P, PASSES, T], U8, "tab_sc")
+        tab2_sc = held([P, T3], U8, "tab2_sc")
+        w4_raw = held([P, PASSES, 512], I32, "w4_raw")
+        w4_sc_raw = held([P, PASSES, 1024], U8, "w4_sc_raw")
+        w4_q = held([P, PASSES * 1024], U16, "w4_q")
+        w4_sc = held([P, PASSES * 1024], U8, "w4_sc")
+        v_q = [held([P, S], U32, "v_q%d" % a) for a in range(PASSES)]
+        v_sc = [held([P, S], U8, "v_sc%d" % a) for a in range(PASSES)]
+        v2_q = [held([P, S2], U32, "v2_q%d" % a) for a in range(PASSES)]
+        v2_sc = held([P, S2], U8, "v2_sc")
+        cap_sb = held([P, PASSES, PACK], F32, "cap_sb")
+        base_sb = held([P, PASSES, PACK], F32, "base_sb")
+        arena_sb = held([P, M_TILES, S], F32, "arena_sb")
+        wgo_sb = held([P, S], F32, "wgo_sb")
+        pages = [held([P, T2], F32, "page%d" % m) for m in range(M_TILES)]
+        pieces = [(b, a) for b in range(PASSES) for a in range(PASSES)]
+        w1_raw = {ba: held([P, PACK, K_PASS], F32, "w1_raw%d%d" % ba) for ba in pieces}
+        w1_bf = {ba: held([P, PACK, P, PACK], BF16, "w1_bf%d%d" % ba) for ba in pieces}
+        w1_q = {ba: held([P, K_PASS], U32, "w1_q%d%d" % ba) for ba in pieces}
+        w1_sc = {ba: held([P, K_PASS], U8, "w1_sc%d%d" % ba) for ba in pieces}
+        lifted = {(b, t): held([P, S], F32, "lifted%d%d" % (b, t)) for b in range(PASSES) for t in range(PACK)}
+        h_planes = [held([P, PACK, S], BF16, "h_planes%d" % b) for b in range(PASSES)]
+        h_bf = [held([P, S, PACK], BF16, "h_bf%d" % b) for b in range(PASSES)]
+        h_q = [held([P, S], U32, "h_q%d" % b) for b in range(PASSES)]
+        h_sc = [held([P, S], U8, "h_sc%d" % b) for b in range(PASSES)]
+
+        nc.vector.memset(tab_sc[:].bitcast(I32), 0)
+        nc.gpsimd.memset(w4_sc_raw[:].bitcast(I32), 0)
+        nc.gpsimd.memset(tab2_sc[:].bitcast(I32), 0)
+
+        def load_words(dst, words, a):
+            nc.sync.dma_start(dst[:], words[a].rearrange("p n t -> p (n t)").bitcast(I32))
+
+        def load_scales_side_by_side(dst, scales):
+            for q in range(4):
+                nc.sync.dma_start(
+                    dst[32 * q : 32 * q + 4, :, :].bitcast(I32),
+                    scales[:, 4 * q : 4 * q + 4, :].rearrange("a r n -> r a n").bitcast(I32),
+                )
+
+        def load_w1(b, a):
+            rows = w1[a * K_PASS : (a + 1) * K_PASS, b * K_PASS : (b + 1) * K_PASS]
+            nc.sync.dma_start(w1_raw[b, a][:], rows.rearrange("(p j) c -> p j c", j=PACK))
+
+        nc.sync.dma_start(w4_raw[:], w4_words.rearrange("a p n -> p a n").bitcast(I32))
+        load_words(tab_sb[0], tab_words, 0)
+        nc.sync.dma_start(ride_list[:], offs)
+        load_scales_side_by_side(tab_sc, tab_scales)
+        load_words(tab_sb[1], tab_words, 1)
+        load_scales_side_by_side(w4_sc_raw, w4_scales)
+        load_w1(0, 0)
+        nc.sync.dma_start(base_sb[:], base.rearrange("(b p t) -> p b t", b=PASSES, t=PACK))
+        nc.sync.dma_start(cap_sb[:], cap.rearrange("(b p t) -> p b t", b=PASSES, t=PACK))
+        load_w1(0, 1)
+        nc.sync.dma_start(bull_list[:], offs2)
+        for q in range(4):
+            nc.sync.dma_start(
+                tab2_sc[32 * q : 32 * q + 4 * PASSES, :].bitcast(I32),
+                tab2_scales[:, 4 * q : 4 * q + 4, :].bitcast(I32),
+            )
+        load_w1(1, 0)
+        load_w1(1, 1)
+        load_words(tab2_sb[0], tab2_words, 0)
+        load_words(tab2_sb[1], tab2_words, 1)
+        nc.sync.dma_start(arena_sb[:], arena.rearrange("(g p) j -> p g j", p=P))
+        nc.sync.dma_start(page_list[:], offs3)
+        nc.sync.dma_start(wgo_sb[:], wgo)
+        for m in range(M_TILES):
+            nc.sync.dma_start(pages[m][:], page1[m * P : (m + 1) * P, :])
+
+        nc.vector.tensor_copy(
+            out=w4_q[:].rearrange("p (g t c i) -> p g c t i", g=4, t=PACK, i=8),
+            in_=w4_raw[:].rearrange("p a n -> p (a n)").bitcast(U16).rearrange("p (g c i t) -> p g c t i", g=4, t=PACK, i=8),
+        )
+        nc.vector.tensor_copy(v_q[0][:], tab_sb[0][:].bitcast(U32).indirect(ride_list[:]))
+        for a in range(PASSES):
+            nc.vector.tensor_copy(v_sc[a][:], tab_sc[:, a, :].indirect(ride_list[:]))
+        nc.vector.tensor_copy(
+            out=w4_sc[:].rearrange("p (g t c i) -> p g c t i", g=4, t=PACK, i=16),
+            in_=w4_sc_raw[:].rearrange("p a n -> p (a n)").rearrange("p (g c i t) -> p g c t i", g=4, t=PACK, i=16),
+        )
+        nc.vector.tensor_copy(v_q[1][:], tab_sb[1][:].bitcast(U32).indirect(ride_list[:]))
+
+        def cast_w1(b, a):
+            nc.scalar.copy(
+                out=w1_bf[b, a][:].rearrange("p t m j -> p m t j"),
+                in_=w1_raw[b, a][:].rearrange("p j (m t) -> p m t j", t=PACK),
+            )
+
+        def quantise_w1(b, a):
+            nc.vector.quantize_mx(
+                out=w1_q[b, a][:].bitcast(FP8X4),
+                scales=w1_sc[b, a][:],
+                in_=w1_bf[b, a][:].rearrange("p t m j -> p (t m j)"),
+            )
+
+        def ride_product(b, weights):
+            banks = [psum.tile([P, S], F32, name="f_bank", tag="f", bufs=4) for t in range(PACK)]
+            for a in range(PASSES):
+                for t in range(PACK):
+                    codes, scales = weights(b, a, t)
+                    nc.tensor.matmul_mx(
+                        out=banks[t][:], lhsT=codes, lhsT_scale=scales,
+                        rhs=v_q[a][:].bitcast(FP8X4), rhs_scale=v_sc[a][:],
+                        start=(a == 0), stop=(a == PASSES - 1),
+                    )
+            return banks
+
+        def w4_slice(b, a, t):
+            c0 = a * 1024 + b * K_PASS + t * P
+            return w4_q[:, c0 : c0 + P].bitcast(FP4X4), w4_sc[:, c0 : c0 + P]
+
+        def w1_slice(b, a, t):
+            return w1_q[b, a][:, t * P : (t + 1) * P].bitcast(FP8X4), w1_sc[b, a][:, t * P : (t + 1) * P]
+
+        def lift(b):
+            banks = ride_product(b, w4_slice)
+            for t in range(PACK):
+                nc.vector.tensor_scalar_max(lifted[b, t][:], banks[t][:], base_sb[:, b, t : t + 1])
+
+        def feature(b):
+            banks = ride_product(b, w1_slice)
+            for t in range(PACK):
+                nc.vector.scalar_tensor_tensor(
+                    out=h_planes[b][:, t, :], in0=banks[t][:], scalar=cap_sb[:, b, t : t + 1],
+                    in1=lifted[b, t][:], op0=ALU.min, op1=ALU.add,
+                )
+            nc.scalar.copy(
+                out=h_bf[b][:].rearrange("p (c i) t -> p c t i", i=4),
+                in_=h_planes[b][:].rearrange("p t (c i) -> p c t i", i=4),
+            )
+
+        def quantise_h(b):
+            nc.vector.quantize_mx(
+                out=h_q[b][:].bitcast(FP8X4), scales=h_sc[b][:],
+                in_=h_bf[b][:].rearrange("p j t -> p (j t)"),
+            )
+
+        cast_w1(0, 0)
+        cast_w1(0, 1)
+        lift(0)
+        quantise_w1(0, 0)
+        lift(1)
+        quantise_w1(0, 1)
+        cast_w1(1, 0)
+        cast_w1(1, 1)
+        feature(0)
+        quantise_w1(1, 0)
+        quantise_w1(1, 1)
+        nc.vector.tensor_copy(v2_sc[:], tab2_sc[:].indirect(bull_list[:]))
+        quantise_h(0)
+        feature(1)
+        for a in range(PASSES):
+            nc.vector.tensor_copy(v2_q[a][:], tab2_sb[a][:].bitcast(U32).indirect(bull_list[:]))
+        quantise_h(1)
+
+        def bull_product(m, codes, scales, tag):
+            bank = psum.tile([P, S], F32, name="bull_bank", tag=tag, bufs=2)
+            for a in range(PASSES):
+                nc.tensor.matmul_mx(
+                    out=bank[:],
+                    lhsT=v2_q[a][:, m * P : (m + 1) * P].bitcast(FP8X4),
+                    lhsT_scale=v2_sc[4 * a : P, m * P : (m + 1) * P],
+                    rhs=codes[a][:].bitcast(FP8X4), rhs_scale=scales[a][:],
+                    start=(a == 0), stop=(a == PASSES - 1),
+                )
+            return bank
+
+        def score(m):
+            d_bank = bull_product(m, v_q, v_sc, "d")
+            e_bank = bull_product(m, h_q, h_sc, "e")
+            weighted = ring.tile([P, S], F32, name="weighted")
+            nc.vector.tensor_tensor(weighted[:], e_bank[:], arena_sb[:, m, :], ALU.mult)
+            summed = ring.tile([P, S], F32, name="summed")
+            nc.vector.tensor_tensor(summed[:], d_bank[:], weighted[:], ALU.add)
+            bounded = ring.tile([P, S], F32, name="bounded")
+            nc.scalar.activation(bounded[:], summed[:], ACT.Tanh)
+            return bounded
+
+        def place(m, bounded):
+            nc.vector.tensor_tensor(pages[m][:].indirect(page_list[:]), bounded[:], wgo_sb[:], ALU.mult)
+            nc.sync.dma_start(out[m * P : (m + 1) * P, :], pages[m][:])
+
+        pending = score(0)
+        for m in range(M_TILES):
+            following = score(m + 1) if m + 1 < M_TILES else None
+            place(m, pending)
+            pending = following

@@ -1,6 +1,7 @@
 from contextlib import ExitStack
 
 import concourse.mybir as mybir
+from concourse.masks import make_identity
 
 F32 = mybir.dt.float32
 BF16 = mybir.dt.bfloat16
@@ -17,9 +18,17 @@ P = 128
 PACK = 4
 K_PASS = P * PACK
 PASSES = 2
-T, T3, S, S2, T2 = 2048, 1024, 512, 512, 1024
+H = PASSES * K_PASS
+T, T3, T2 = 2048, 1024, 1024
+S, S2 = 512, 512
 M_TILES = S2 // P
-FLOPS = 3221225472
+J_TILES = S // P
+LIST_ROWS = 16
+QUADRANTS, QUADRANT = 4, 32
+SCALE_ROWS = 4
+LINE = 16
+BANKS = 8
+FLOPS = 2 * 2 * H * H * S + 2 * 2 * H * S2 * S
 
 
 def tile_list_bull_ride_scores_kernel(
@@ -29,26 +38,26 @@ def tile_list_bull_ride_scores_kernel(
     nc = tc.nc
     with ExitStack() as ctx:
         keep = ctx.enter_context(tc.tile_pool(name="keep", bufs=1))
-        ring = ctx.enter_context(tc.tile_pool(name="ring", bufs=2))
+        ring = ctx.enter_context(tc.tile_pool(name="ring", bufs=M_TILES))
         psum = ctx.enter_context(tc.psum_pool(name="psum", bufs=1))
 
-        def held(shape, dtype, name):
-            return keep.tile(shape, dtype, name=name, align_bytes=64)
+        def held(shape, dtype, name, tag=None):
+            return keep.tile(shape, dtype, name=name, tag=tag or name, align_bytes=64)
 
-        ride_list = held([P, S // 16], U16, "ride_list")
-        bull_list = held([P, S2 // 16], U16, "bull_list")
-        page_list = held([P, S // 16], U16, "page_list")
+        ride_list = held([P, S // LIST_ROWS], U16, "ride_list")
+        bull_list = held([P, S2 // LIST_ROWS], U16, "bull_list")
+        page_list = held([P, S // LIST_ROWS], U16, "page_list")
         tab_sb = [held([P, T], I32, "tab_sb%d" % a) for a in range(PASSES)]
         tab2_sb = [held([P, T3], I32, "tab2_sb%d" % a) for a in range(PASSES)]
         tab_sc = held([P, PASSES, T], U8, "tab_sc")
         tab2_sc = held([P, T3], U8, "tab2_sc")
-        w4_raw = held([P, PASSES, 512], I32, "w4_raw")
-        w4_sc_raw = held([P, PASSES, 1024], U8, "w4_sc_raw")
-        w4_q = held([P, PASSES * 1024], U16, "w4_q")
-        w4_sc = held([P, PASSES * 1024], U8, "w4_sc")
+        w4_raw = held([P, PASSES, H // 2], I32, "w4_raw")
+        w4_sc_raw = held([P, PASSES, H], U8, "w4_sc_raw")
+        w4_q = held([P, PASSES * H], U16, "w4_q")
+        w4_sc = held([P, PASSES * H], U8, "w4_sc")
         v_q = [held([P, S], U32, "v_q%d" % a) for a in range(PASSES)]
         v_sc = [held([P, S], U8, "v_sc%d" % a) for a in range(PASSES)]
-        v2_q = [held([P, S2], U32, "v2_q%d" % a) for a in range(PASSES)]
+        warm = held([P, 2], F32, "warm")
         v2_sc = held([P, S2], U8, "v2_sc")
         cap_sb = held([P, PASSES, PACK], F32, "cap_sb")
         base_sb = held([P, PASSES, PACK], F32, "base_sb")
@@ -58,86 +67,102 @@ def tile_list_bull_ride_scores_kernel(
         pieces = [(b, a) for b in range(PASSES) for a in range(PASSES)]
         w1_raw = {ba: held([P, PACK, K_PASS], F32, "w1_raw%d%d" % ba) for ba in pieces}
         w1_bf = {ba: held([P, PACK, P, PACK], BF16, "w1_bf%d%d" % ba) for ba in pieces}
-        w1_q = {ba: held([P, K_PASS], U32, "w1_q%d%d" % ba) for ba in pieces}
+        w1_q = {}
         w1_sc = {ba: held([P, K_PASS], U8, "w1_sc%d%d" % ba) for ba in pieces}
         lifted = {(b, t): held([P, S], F32, "lifted%d%d" % (b, t)) for b in range(PASSES) for t in range(PACK)}
         h_planes = [held([P, PACK, S], BF16, "h_planes%d" % b) for b in range(PASSES)]
-        h_bf = [held([P, S, PACK], BF16, "h_bf%d" % b) for b in range(PASSES)]
         h_q = [held([P, S], U32, "h_q%d" % b) for b in range(PASSES)]
         h_sc = [held([P, S], U8, "h_sc%d" % b) for b in range(PASSES)]
 
         nc.vector.memset(tab_sc[:].bitcast(I32), 0)
         nc.gpsimd.memset(w4_sc_raw[:].bitcast(I32), 0)
-        nc.gpsimd.memset(tab2_sc[:].bitcast(I32), 0)
+        nc.vector.memset(warm[:, 0:1], 0.0)
+        nc.vector.memset(tab2_sc[:].bitcast(I32), 0)
+        nc.scalar.activation(warm[:, 1:2], warm[:, 0:1], ACT.Tanh)
+        identity = held([P, P], F32, "identity")
+        make_identity(nc, identity[:])
 
         def load_words(dst, words, a):
             nc.sync.dma_start(dst[:], words[a].rearrange("p n t -> p (n t)").bitcast(I32))
 
-        def load_scales_side_by_side(dst, scales):
-            for q in range(4):
+        def load_scales_packed(dst, scales):
+            for q in range(QUADRANTS):
                 nc.sync.dma_start(
-                    dst[32 * q : 32 * q + 4, :, :].bitcast(I32),
-                    scales[:, 4 * q : 4 * q + 4, :].rearrange("a r n -> r a n").bitcast(I32),
+                    dst[QUADRANT * q : QUADRANT * q + SCALE_ROWS * PASSES, :].bitcast(I32),
+                    scales[:, SCALE_ROWS * q : SCALE_ROWS * (q + 1), :].bitcast(I32),
+                )
+
+        def load_scales_side_by_side(dst, scales):
+            for q in range(QUADRANTS):
+                nc.sync.dma_start(
+                    dst[QUADRANT * q : QUADRANT * q + SCALE_ROWS, :, :].bitcast(I32),
+                    scales[:, SCALE_ROWS * q : SCALE_ROWS * (q + 1), :].rearrange("a s n -> s a n").bitcast(I32),
                 )
 
         def load_w1(b, a):
             rows = w1[a * K_PASS : (a + 1) * K_PASS, b * K_PASS : (b + 1) * K_PASS]
-            nc.sync.dma_start(w1_raw[b, a][:], rows.rearrange("(p j) c -> p j c", j=PACK))
+            nc.sync.dma_start(w1_raw[b, a][:], rows.rearrange("(p i) c -> p i c", i=PACK))
 
         nc.sync.dma_start(w4_raw[:], w4_words.rearrange("a p n -> p a n").bitcast(I32))
-        load_words(tab_sb[0], tab_words, 0)
         nc.sync.dma_start(ride_list[:], offs)
-        load_scales_side_by_side(tab_sc, tab_scales)
-        load_words(tab_sb[1], tab_words, 1)
-        load_scales_side_by_side(w4_sc_raw, w4_scales)
-        load_w1(0, 0)
         nc.sync.dma_start(base_sb[:], base.rearrange("(b p t) -> p b t", b=PASSES, t=PACK))
-        nc.sync.dma_start(cap_sb[:], cap.rearrange("(b p t) -> p b t", b=PASSES, t=PACK))
-        load_w1(0, 1)
+        load_scales_side_by_side(tab_sc, tab_scales)
+        load_words(tab_sb[0], tab_words, 0)
+        load_scales_side_by_side(w4_sc_raw, w4_scales)
+        load_words(tab_sb[1], tab_words, 1)
+        load_w1(0, 0)
         nc.sync.dma_start(bull_list[:], offs2)
-        for q in range(4):
-            nc.sync.dma_start(
-                tab2_sc[32 * q : 32 * q + 4 * PASSES, :].bitcast(I32),
-                tab2_scales[:, 4 * q : 4 * q + 4, :].bitcast(I32),
-            )
+        load_scales_packed(tab2_sc, tab2_scales)
+        load_w1(0, 1)
+        nc.sync.dma_start(cap_sb[:], cap.rearrange("(b p t) -> p b t", b=PASSES, t=PACK))
         load_w1(1, 0)
         load_w1(1, 1)
+        nc.sync.dma_start(page_list[:], offs3)
         load_words(tab2_sb[0], tab2_words, 0)
         load_words(tab2_sb[1], tab2_words, 1)
         nc.sync.dma_start(arena_sb[:], arena.rearrange("(g p) j -> p g j", p=P))
-        nc.sync.dma_start(page_list[:], offs3)
         nc.sync.dma_start(wgo_sb[:], wgo)
         for m in range(M_TILES):
             nc.sync.dma_start(pages[m][:], page1[m * P : (m + 1) * P, :])
 
         nc.vector.tensor_copy(
-            out=w4_q[:].rearrange("p (g t c i) -> p g c t i", g=4, t=PACK, i=8),
-            in_=w4_raw[:].rearrange("p a n -> p (a n)").bitcast(U16).rearrange("p (g c i t) -> p g c t i", g=4, t=PACK, i=8),
+            out=w4_q[:].rearrange("p (g t c i) -> p g c t i", g=PASSES * PASSES, t=PACK, i=LINE // 2),
+            in_=w4_raw[:].rearrange("p a n -> p (a n)").bitcast(U16).rearrange(
+                "p (g c i t) -> p g c t i", g=PASSES * PASSES, t=PACK, i=LINE // 2
+            ),
         )
-        nc.vector.tensor_copy(v_q[0][:], tab_sb[0][:].bitcast(U32).indirect(ride_list[:]))
-        for a in range(PASSES):
+
+        def deal_w4_scales(b):
+            nc.vector.tensor_copy(
+                out=w4_sc[:].rearrange("p (a b t c i) -> p b a c t i", a=PASSES, b=PASSES, t=PACK, i=LINE)[:, b],
+                in_=w4_sc_raw[:].rearrange("p a (b c i t) -> p b a c t i", b=PASSES, t=PACK, i=LINE)[:, b],
+            )
+
+        def gather_rides(a):
             nc.vector.tensor_copy(v_sc[a][:], tab_sc[:, a, :].indirect(ride_list[:]))
-        nc.vector.tensor_copy(
-            out=w4_sc[:].rearrange("p (g t c i) -> p g c t i", g=4, t=PACK, i=16),
-            in_=w4_sc_raw[:].rearrange("p a n -> p (a n)").rearrange("p (g c i t) -> p g c t i", g=4, t=PACK, i=16),
-        )
-        nc.vector.tensor_copy(v_q[1][:], tab_sb[1][:].bitcast(U32).indirect(ride_list[:]))
+            nc.vector.tensor_copy(v_q[a][:], tab_sb[a][:].bitcast(U32).indirect(ride_list[:]))
+
+        deal_w4_scales(0)
+        gather_rides(0)
+        gather_rides(1)
+        deal_w4_scales(1)
 
         def cast_w1(b, a):
             nc.scalar.copy(
-                out=w1_bf[b, a][:].rearrange("p t m j -> p m t j"),
-                in_=w1_raw[b, a][:].rearrange("p j (m t) -> p m t j", t=PACK),
+                out=w1_bf[b, a][:].rearrange("p t m i -> p m t i"),
+                in_=w1_raw[b, a][:].rearrange("p i (m t) -> p m t i", t=PACK),
             )
 
-        def quantise_w1(b, a):
+        def quantise_w1(b, a, tag=None):
+            w1_q[b, a] = held([P, K_PASS], U32, "w1_q%d%d" % (b, a), tag=tag)
             nc.vector.quantize_mx(
                 out=w1_q[b, a][:].bitcast(FP8X4),
                 scales=w1_sc[b, a][:],
-                in_=w1_bf[b, a][:].rearrange("p t m j -> p (t m j)"),
+                in_=w1_bf[b, a][:].rearrange("p t m i -> p (t m i)"),
             )
 
         def ride_product(b, weights):
-            banks = [psum.tile([P, S], F32, name="f_bank", tag="f", bufs=4) for t in range(PACK)]
+            banks = [psum.tile([P, S], F32, name="f_bank", tag="bank", bufs=BANKS) for t in range(PACK)]
             for a in range(PASSES):
                 for t in range(PACK):
                     codes, scales = weights(b, a, t)
@@ -149,7 +174,7 @@ def tile_list_bull_ride_scores_kernel(
             return banks
 
         def w4_slice(b, a, t):
-            c0 = a * 1024 + b * K_PASS + t * P
+            c0 = a * H + b * K_PASS + t * P
             return w4_q[:, c0 : c0 + P].bitcast(FP4X4), w4_sc[:, c0 : c0 + P]
 
         def w1_slice(b, a, t):
@@ -160,71 +185,111 @@ def tile_list_bull_ride_scores_kernel(
             for t in range(PACK):
                 nc.vector.tensor_scalar_max(lifted[b, t][:], banks[t][:], base_sb[:, b, t : t + 1])
 
-        def feature(b):
-            banks = ride_product(b, w1_slice)
-            for t in range(PACK):
-                nc.vector.scalar_tensor_tensor(
-                    out=h_planes[b][:, t, :], in0=banks[t][:], scalar=cap_sb[:, b, t : t + 1],
-                    in1=lifted[b, t][:], op0=ALU.min, op1=ALU.add,
+        h_bf = []
+
+        def feature(b, banks, parts):
+            h_bf.append(held([P, S, PACK], BF16, "h_bf%d" % b, tag="w1_raw1%d" % (1 - b)))
+            width = S // parts
+            for part in range(parts):
+                cols = slice(part * width, (part + 1) * width)
+                for t in range(PACK):
+                    nc.vector.scalar_tensor_tensor(
+                        out=h_planes[b][:, t, cols], in0=banks[t][:, cols], scalar=cap_sb[:, b, t : t + 1],
+                        in1=lifted[b, t][:, cols], op0=ALU.min, op1=ALU.add,
+                    )
+                nc.scalar.copy(
+                    out=h_bf[b][:, cols, :].rearrange("p (c i) t -> p c t i", i=PACK),
+                    in_=h_planes[b][:, :, cols].rearrange("p t (c i) -> p c t i", i=PACK),
                 )
-            nc.scalar.copy(
-                out=h_bf[b][:].rearrange("p (c i) t -> p c t i", i=4),
-                in_=h_planes[b][:].rearrange("p t (c i) -> p c t i", i=4),
-            )
 
-        def quantise_h(b):
-            nc.vector.quantize_mx(
-                out=h_q[b][:].bitcast(FP8X4), scales=h_sc[b][:],
-                in_=h_bf[b][:].rearrange("p j t -> p (j t)"),
-            )
+        def quantise_h(b, parts):
+            width = S // parts
+            for part in range(parts):
+                cols = slice(part * width, (part + 1) * width)
+                nc.vector.quantize_mx(
+                    out=h_q[b][:, cols].bitcast(FP8X4), scales=h_sc[b][:, cols],
+                    in_=h_bf[b][:, cols, :].rearrange("p j t -> p (j t)"),
+                )
 
+        def gather_bulls(a, tag):
+            v2_q.append(held([P, S2], U32, "v2_q%d" % a, tag=tag))
+            nc.vector.tensor_copy(v2_q[a][:], tab2_sb[a][:].bitcast(U32).indirect(bull_list[:]))
+
+        def new_bank(name):
+            return psum.tile([P, J_TILES, P], F32, name=name, tag="bank", bufs=BANKS)
+
+        def turned_pass(bank, m, a, codes, scales):
+            for g in range(J_TILES):
+                nc.tensor.matmul_mx(
+                    out=bank[:, g, :],
+                    lhsT=codes[a][:, g * P : (g + 1) * P].bitcast(FP8X4),
+                    lhsT_scale=scales[a][:, g * P : (g + 1) * P],
+                    rhs=v2_q[a][:, m * P : (m + 1) * P].bitcast(FP8X4),
+                    rhs_scale=v2_sc[SCALE_ROWS * a : P, m * P : (m + 1) * P],
+                    start=(a == 0 and g == 0), stop=(a == PASSES - 1 and g == J_TILES - 1),
+                )
+
+        def turn_arena(m):
+            bank = new_bank("arena_bank")
+            for g in range(J_TILES):
+                nc.tensor.transpose(bank[:, g, :], arena_sb[:, m, g * P : (g + 1) * P], identity[:])
+            turned = ring.tile([P, J_TILES, P], F32, name="arena_t")
+            nc.scalar.copy(turned[:], bank[:])
+            return turned
+
+        def direct(m):
+            bank = new_bank("d_bank")
+            for a in range(PASSES):
+                turned_pass(bank, m, a, v_q, v_sc)
+            turned = ring.tile([P, J_TILES, P], F32, name="d_t")
+            nc.scalar.copy(turned[:], bank[:])
+            return turned
+
+        def weigh(m, turned_arena):
+            bank = new_bank("e_bank")
+            for a in range(PASSES):
+                turned_pass(bank, m, a, h_q, h_sc)
+            product = ring.tile([P, J_TILES, P], F32, name="weighted")
+            nc.vector.tensor_tensor(product[:], bank[:], turned_arena[:], ALU.mult)
+            return product
+
+        def bound(terms):
+            bank = new_bank("sum_bank")
+            for n, term in enumerate(terms):
+                for g in range(J_TILES):
+                    nc.tensor.matmul(
+                        bank[:, g, :], term[:, g, :], identity[:], is_transpose=True,
+                        start=(n == 0 and g == 0), stop=(n == len(terms) - 1 and g == J_TILES - 1),
+                    )
+            scores = ring.tile([P, S], F32, name="bounded")
+            nc.scalar.activation(scores[:], bank[:].rearrange("p g j -> p (g j)"), ACT.Tanh)
+            return scores
+
+        v2_q = []
         cast_w1(0, 0)
         cast_w1(0, 1)
         lift(0)
         quantise_w1(0, 0)
-        lift(1)
         quantise_w1(0, 1)
+        lift(1)
+        nc.vector.tensor_copy(v2_sc[:], tab2_sc[:].indirect(bull_list[:]))
         cast_w1(1, 0)
         cast_w1(1, 1)
-        feature(0)
-        quantise_w1(1, 0)
-        quantise_w1(1, 1)
-        nc.vector.tensor_copy(v2_sc[:], tab2_sc[:].indirect(bull_list[:]))
-        quantise_h(0)
-        feature(1)
-        for a in range(PASSES):
-            nc.vector.tensor_copy(v2_q[a][:], tab2_sb[a][:].bitcast(U32).indirect(bull_list[:]))
-        quantise_h(1)
-
-        def bull_product(m, codes, scales, tag):
-            bank = psum.tile([P, S], F32, name="bull_bank", tag=tag, bufs=2)
-            for a in range(PASSES):
-                nc.tensor.matmul_mx(
-                    out=bank[:],
-                    lhsT=v2_q[a][:, m * P : (m + 1) * P].bitcast(FP8X4),
-                    lhsT_scale=v2_sc[4 * a : P, m * P : (m + 1) * P],
-                    rhs=codes[a][:].bitcast(FP8X4), rhs_scale=scales[a][:],
-                    start=(a == 0), stop=(a == PASSES - 1),
-                )
-            return bank
-
-        def score(m):
-            d_bank = bull_product(m, v_q, v_sc, "d")
-            e_bank = bull_product(m, h_q, h_sc, "e")
-            weighted = ring.tile([P, S], F32, name="weighted")
-            nc.vector.tensor_tensor(weighted[:], e_bank[:], arena_sb[:, m, :], ALU.mult)
-            summed = ring.tile([P, S], F32, name="summed")
-            nc.vector.tensor_tensor(summed[:], d_bank[:], weighted[:], ALU.add)
-            bounded = ring.tile([P, S], F32, name="bounded")
-            nc.scalar.activation(bounded[:], summed[:], ACT.Tanh)
-            return bounded
-
-        def place(m, bounded):
+        feature(0, ride_product(0, w1_slice), 1)
+        quantise_w1(1, 0, "lifted00")
+        quantise_w1(1, 1, "lifted01")
+        gather_bulls(0, "lifted02")
+        gather_bulls(1, "lifted03")
+        last_banks = ride_product(1, w1_slice)
+        arena_t = [turn_arena(m) for m in range(M_TILES // 2)]
+        d_t = [direct(0)]
+        feature(1, last_banks, 2)
+        quantise_h(0, 1)
+        quantise_h(1, 2)
+        arena_t.extend(turn_arena(m) for m in range(M_TILES // 2, M_TILES))
+        d_t.extend(direct(m) for m in range(1, M_TILES))
+        weighted = [weigh(m, arena_t[m]) for m in range(M_TILES)]
+        for m in range(M_TILES):
+            bounded = bound([d_t[m], weighted[m]])
             nc.vector.tensor_tensor(pages[m][:].indirect(page_list[:]), bounded[:], wgo_sb[:], ALU.mult)
             nc.sync.dma_start(out[m * P : (m + 1) * P, :], pages[m][:])
-
-        pending = score(0)
-        for m in range(M_TILES):
-            following = score(m + 1) if m + 1 < M_TILES else None
-            place(m, pending)
-            pending = following

from contextlib import ExitStack

import concourse.mybir as mybir
from concourse.masks import make_identity

F32 = mybir.dt.float32
BF16 = mybir.dt.bfloat16
I32 = mybir.dt.int32
U32 = mybir.dt.uint32
U16 = mybir.dt.uint16
U8 = mybir.dt.uint8
FP8X4 = mybir.dt.float8_e4m3fn_x4
FP4X4 = mybir.dt.float4_e2m1fn_x4
ALU = mybir.AluOpType
ACT = mybir.ActivationFunctionType

P = 128
PACK = 4
K_PASS = P * PACK
PASSES = 2
H = PASSES * K_PASS
T, T3, T2 = 2048, 1024, 1024
S, S2 = 512, 512
M_TILES = S2 // P
J_TILES = S // P
LIST_ROWS = 16
QUADRANTS, QUADRANT = 4, 32
SCALE_ROWS = 4
LINE = 16
BANKS = 8
FLOPS = 2 * 2 * H * H * S + 2 * 2 * H * S2 * S


def tile_list_bull_ride_scores_kernel(
    tc, tab_words, tab_scales, offs, tab2_words, tab2_scales, offs2, offs3,
    w1, w4_words, w4_scales, cap, base, arena, page1, wgo, out,
):
    nc = tc.nc
    with ExitStack() as ctx:
        keep = ctx.enter_context(tc.tile_pool(name="keep", bufs=1))
        ring = ctx.enter_context(tc.tile_pool(name="ring", bufs=M_TILES))
        psum = ctx.enter_context(tc.psum_pool(name="psum", bufs=1))

        def held(shape, dtype, name, tag=None):
            return keep.tile(shape, dtype, name=name, tag=tag or name, align_bytes=64)

        ride_list = held([P, S // LIST_ROWS], U16, "ride_list")
        bull_list = held([P, S2 // LIST_ROWS], U16, "bull_list")
        page_list = held([P, S // LIST_ROWS], U16, "page_list")
        tab_sb = [held([P, T], I32, "tab_sb%d" % a) for a in range(PASSES)]
        tab2_sb = [held([P, T3], I32, "tab2_sb%d" % a) for a in range(PASSES)]
        tab_sc = held([P, PASSES, T], U8, "tab_sc")
        tab2_sc = held([P, T3], U8, "tab2_sc")
        w4_raw = held([P, PASSES, H // 2], I32, "w4_raw")
        w4_sc_raw = held([P, PASSES, H], U8, "w4_sc_raw")
        w4_q = held([P, PASSES * H], U16, "w4_q")
        w4_sc = held([P, PASSES * H], U8, "w4_sc")
        v_q = [held([P, S], U32, "v_q%d" % a) for a in range(PASSES)]
        v_sc = [held([P, S], U8, "v_sc%d" % a) for a in range(PASSES)]
        warm = held([P, 2], F32, "warm")
        v2_sc = held([P, S2], U8, "v2_sc")
        cap_sb = held([P, PASSES, PACK], F32, "cap_sb")
        base_sb = held([P, PASSES, PACK], F32, "base_sb")
        arena_sb = held([P, M_TILES, S], F32, "arena_sb")
        wgo_sb = held([P, S], F32, "wgo_sb")
        pages = [held([P, T2], F32, "page%d" % m) for m in range(M_TILES)]
        pieces = [(b, a) for b in range(PASSES) for a in range(PASSES)]
        w1_raw = {ba: held([P, PACK, K_PASS], F32, "w1_raw%d%d" % ba) for ba in pieces}
        w1_bf = {ba: held([P, PACK, P, PACK], BF16, "w1_bf%d%d" % ba) for ba in pieces}
        w1_q = {}
        w1_sc = {ba: held([P, K_PASS], U8, "w1_sc%d%d" % ba) for ba in pieces}
        lifted = {(b, t): held([P, S], F32, "lifted%d%d" % (b, t)) for b in range(PASSES) for t in range(PACK)}
        h_planes = [held([P, PACK, S], BF16, "h_planes%d" % b) for b in range(PASSES)]
        h_q = [held([P, S], U32, "h_q%d" % b) for b in range(PASSES)]
        h_sc = [held([P, S], U8, "h_sc%d" % b) for b in range(PASSES)]

        nc.vector.memset(tab_sc[:].bitcast(I32), 0)
        nc.gpsimd.memset(w4_sc_raw[:].bitcast(I32), 0)
        nc.vector.memset(warm[:, 0:1], 0.0)
        nc.vector.memset(tab2_sc[:].bitcast(I32), 0)
        nc.scalar.activation(warm[:, 1:2], warm[:, 0:1], ACT.Tanh)
        identity = held([P, P], F32, "identity")
        make_identity(nc, identity[:])

        def load_words(dst, words, a):
            nc.sync.dma_start(dst[:], words[a].rearrange("p n t -> p (n t)").bitcast(I32))

        def load_scales_packed(dst, scales):
            for q in range(QUADRANTS):
                nc.sync.dma_start(
                    dst[QUADRANT * q : QUADRANT * q + SCALE_ROWS * PASSES, :].bitcast(I32),
                    scales[:, SCALE_ROWS * q : SCALE_ROWS * (q + 1), :].bitcast(I32),
                )

        def load_scales_side_by_side(dst, scales):
            for q in range(QUADRANTS):
                nc.sync.dma_start(
                    dst[QUADRANT * q : QUADRANT * q + SCALE_ROWS, :, :].bitcast(I32),
                    scales[:, SCALE_ROWS * q : SCALE_ROWS * (q + 1), :].rearrange("a s n -> s a n").bitcast(I32),
                )

        def load_w1(b, a):
            rows = w1[a * K_PASS : (a + 1) * K_PASS, b * K_PASS : (b + 1) * K_PASS]
            nc.sync.dma_start(w1_raw[b, a][:], rows.rearrange("(p i) c -> p i c", i=PACK))

        nc.sync.dma_start(w4_raw[:], w4_words.rearrange("a p n -> p a n").bitcast(I32))
        nc.sync.dma_start(ride_list[:], offs)
        nc.sync.dma_start(base_sb[:], base.rearrange("(b p t) -> p b t", b=PASSES, t=PACK))
        load_scales_side_by_side(tab_sc, tab_scales)
        load_words(tab_sb[0], tab_words, 0)
        load_scales_side_by_side(w4_sc_raw, w4_scales)
        load_words(tab_sb[1], tab_words, 1)
        load_w1(0, 0)
        nc.sync.dma_start(bull_list[:], offs2)
        load_scales_packed(tab2_sc, tab2_scales)
        load_w1(0, 1)
        nc.sync.dma_start(cap_sb[:], cap.rearrange("(b p t) -> p b t", b=PASSES, t=PACK))
        load_w1(1, 0)
        load_w1(1, 1)
        nc.sync.dma_start(page_list[:], offs3)
        load_words(tab2_sb[0], tab2_words, 0)
        load_words(tab2_sb[1], tab2_words, 1)
        nc.sync.dma_start(arena_sb[:], arena.rearrange("(g p) j -> p g j", p=P))
        nc.sync.dma_start(wgo_sb[:], wgo)
        for m in range(M_TILES):
            nc.sync.dma_start(pages[m][:], page1[m * P : (m + 1) * P, :])

        nc.vector.tensor_copy(
            out=w4_q[:].rearrange("p (g t c i) -> p g c t i", g=PASSES * PASSES, t=PACK, i=LINE // 2),
            in_=w4_raw[:].rearrange("p a n -> p (a n)").bitcast(U16).rearrange(
                "p (g c i t) -> p g c t i", g=PASSES * PASSES, t=PACK, i=LINE // 2
            ),
        )

        def deal_w4_scales(b):
            nc.vector.tensor_copy(
                out=w4_sc[:].rearrange("p (a b t c i) -> p b a c t i", a=PASSES, b=PASSES, t=PACK, i=LINE)[:, b],
                in_=w4_sc_raw[:].rearrange("p a (b c i t) -> p b a c t i", b=PASSES, t=PACK, i=LINE)[:, b],
            )

        def gather_rides(a):
            nc.vector.tensor_copy(v_sc[a][:], tab_sc[:, a, :].indirect(ride_list[:]))
            nc.vector.tensor_copy(v_q[a][:], tab_sb[a][:].bitcast(U32).indirect(ride_list[:]))

        deal_w4_scales(0)
        gather_rides(0)
        gather_rides(1)
        deal_w4_scales(1)

        def cast_w1(b, a):
            nc.scalar.copy(
                out=w1_bf[b, a][:].rearrange("p t m i -> p m t i"),
                in_=w1_raw[b, a][:].rearrange("p i (m t) -> p m t i", t=PACK),
            )

        def quantise_w1(b, a, tag=None):
            w1_q[b, a] = held([P, K_PASS], U32, "w1_q%d%d" % (b, a), tag=tag)
            nc.vector.quantize_mx(
                out=w1_q[b, a][:].bitcast(FP8X4),
                scales=w1_sc[b, a][:],
                in_=w1_bf[b, a][:].rearrange("p t m i -> p (t m i)"),
            )

        def ride_product(b, weights):
            banks = [psum.tile([P, S], F32, name="f_bank", tag="bank", bufs=BANKS) for t in range(PACK)]
            for a in range(PASSES):
                for t in range(PACK):
                    codes, scales = weights(b, a, t)
                    nc.tensor.matmul_mx(
                        out=banks[t][:], lhsT=codes, lhsT_scale=scales,
                        rhs=v_q[a][:].bitcast(FP8X4), rhs_scale=v_sc[a][:],
                        start=(a == 0), stop=(a == PASSES - 1),
                    )
            return banks

        def w4_slice(b, a, t):
            c0 = a * H + b * K_PASS + t * P
            return w4_q[:, c0 : c0 + P].bitcast(FP4X4), w4_sc[:, c0 : c0 + P]

        def w1_slice(b, a, t):
            return w1_q[b, a][:, t * P : (t + 1) * P].bitcast(FP8X4), w1_sc[b, a][:, t * P : (t + 1) * P]

        def lift(b):
            banks = ride_product(b, w4_slice)
            for t in range(PACK):
                nc.vector.tensor_scalar_max(lifted[b, t][:], banks[t][:], base_sb[:, b, t : t + 1])

        h_bf = []

        def feature(b, banks, parts):
            h_bf.append(held([P, S, PACK], BF16, "h_bf%d" % b, tag="w1_raw1%d" % (1 - b)))
            width = S // parts
            for part in range(parts):
                cols = slice(part * width, (part + 1) * width)
                for t in range(PACK):
                    nc.vector.scalar_tensor_tensor(
                        out=h_planes[b][:, t, cols], in0=banks[t][:, cols], scalar=cap_sb[:, b, t : t + 1],
                        in1=lifted[b, t][:, cols], op0=ALU.min, op1=ALU.add,
                    )
                nc.scalar.copy(
                    out=h_bf[b][:, cols, :].rearrange("p (c i) t -> p c t i", i=PACK),
                    in_=h_planes[b][:, :, cols].rearrange("p t (c i) -> p c t i", i=PACK),
                )

        def quantise_h(b, parts):
            width = S // parts
            for part in range(parts):
                cols = slice(part * width, (part + 1) * width)
                nc.vector.quantize_mx(
                    out=h_q[b][:, cols].bitcast(FP8X4), scales=h_sc[b][:, cols],
                    in_=h_bf[b][:, cols, :].rearrange("p j t -> p (j t)"),
                )

        def gather_bulls(a, tag):
            v2_q.append(held([P, S2], U32, "v2_q%d" % a, tag=tag))
            nc.vector.tensor_copy(v2_q[a][:], tab2_sb[a][:].bitcast(U32).indirect(bull_list[:]))

        def new_bank(name):
            return psum.tile([P, J_TILES, P], F32, name=name, tag="bank", bufs=BANKS)

        def turned_pass(bank, m, a, codes, scales):
            for g in range(J_TILES):
                nc.tensor.matmul_mx(
                    out=bank[:, g, :],
                    lhsT=codes[a][:, g * P : (g + 1) * P].bitcast(FP8X4),
                    lhsT_scale=scales[a][:, g * P : (g + 1) * P],
                    rhs=v2_q[a][:, m * P : (m + 1) * P].bitcast(FP8X4),
                    rhs_scale=v2_sc[SCALE_ROWS * a : P, m * P : (m + 1) * P],
                    start=(a == 0 and g == 0), stop=(a == PASSES - 1 and g == J_TILES - 1),
                )

        def turn_arena(m):
            bank = new_bank("arena_bank")
            for g in range(J_TILES):
                nc.tensor.transpose(bank[:, g, :], arena_sb[:, m, g * P : (g + 1) * P], identity[:])
            turned = ring.tile([P, J_TILES, P], F32, name="arena_t")
            nc.scalar.copy(turned[:], bank[:])
            return turned

        def direct(m):
            bank = new_bank("d_bank")
            for a in range(PASSES):
                turned_pass(bank, m, a, v_q, v_sc)
            turned = ring.tile([P, J_TILES, P], F32, name="d_t")
            nc.scalar.copy(turned[:], bank[:])
            return turned

        def weigh(m, turned_arena):
            bank = new_bank("e_bank")
            for a in range(PASSES):
                turned_pass(bank, m, a, h_q, h_sc)
            product = ring.tile([P, J_TILES, P], F32, name="weighted")
            nc.vector.tensor_tensor(product[:], bank[:], turned_arena[:], ALU.mult)
            return product

        def bound(terms):
            bank = new_bank("sum_bank")
            for n, term in enumerate(terms):
                for g in range(J_TILES):
                    nc.tensor.matmul(
                        bank[:, g, :], term[:, g, :], identity[:], is_transpose=True,
                        start=(n == 0 and g == 0), stop=(n == len(terms) - 1 and g == J_TILES - 1),
                    )
            scores = ring.tile([P, S], F32, name="bounded")
            nc.scalar.activation(scores[:], bank[:].rearrange("p g j -> p (g j)"), ACT.Tanh)
            return scores

        v2_q = []
        cast_w1(0, 0)
        cast_w1(0, 1)
        lift(0)
        quantise_w1(0, 0)
        quantise_w1(0, 1)
        lift(1)
        nc.vector.tensor_copy(v2_sc[:], tab2_sc[:].indirect(bull_list[:]))
        cast_w1(1, 0)
        cast_w1(1, 1)
        feature(0, ride_product(0, w1_slice), 1)
        quantise_w1(1, 0, "lifted00")
        quantise_w1(1, 1, "lifted01")
        gather_bulls(0, "lifted02")
        gather_bulls(1, "lifted03")
        last_banks = ride_product(1, w1_slice)
        arena_t = [turn_arena(m) for m in range(M_TILES // 2)]
        d_t = [direct(0)]
        feature(1, last_banks, 2)
        quantise_h(0, 1)
        quantise_h(1, 2)
        arena_t.extend(turn_arena(m) for m in range(M_TILES // 2, M_TILES))
        d_t.extend(direct(m) for m in range(1, M_TILES))
        weighted = [weigh(m, arena_t[m]) for m in range(M_TILES)]
        for m in range(M_TILES):
            bounded = bound([d_t[m], weighted[m]])
            nc.vector.tensor_tensor(pages[m][:].indirect(page_list[:]), bounded[:], wgo_sb[:], ALU.mult)
            nc.sync.dma_start(out[m * P : (m + 1) * P, :], pages[m][:])
